import numpy as np
import ml_dtypes


def mxq(x, axis, fmt="e4m3"):
    dtype, down = {"e4m3": (ml_dtypes.float8_e4m3fn, 7), "e5m2": (ml_dtypes.float8_e5m2, 14)}[fmt]
    v = np.moveaxis(np.asarray(x, np.float32).astype(ml_dtypes.bfloat16).astype(np.float64), axis, -1)
    blocks = v.reshape(v.shape[:-1] + (-1, 32))
    amax = np.abs(blocks).max(-1, keepdims=True)
    byte = np.maximum(np.where(amax > 0, np.frexp(amax)[1] - 1 + 127, 0) - down, 1)
    scale = np.exp2(byte - 127.0)
    codes = (blocks / scale).astype(np.float32).astype(dtype).astype(np.float64)
    return np.moveaxis((codes * scale).reshape(v.shape), -1, axis)


WIDE = False


def mx_kscale(k):
    if not WIDE:
        return np.ones(k)
    levels = np.array([10, -10, 5, -5, 0])
    if k % 512:
        return np.exp2(np.random.permutation(np.resize(levels, k // 32))).repeat(32)
    a = np.empty((k // 512, 16))
    for p in range(k // 512):
        a[p, :8] = np.random.permutation(np.resize(levels, 8))
        for g in range(8):
            far = levels[np.abs(levels - a[p, g]) >= 10]
            a[p, g + 8] = far[np.random.randint(len(far))]
    return np.exp2(a.ravel()).repeat(32)


def f64(x):
    return np.asarray(x).astype(np.float64)


def striped(idx):
    return np.tile(idx.reshape(-1, 16).T, (8, 1)).astype(np.uint16)


def unstriped(offs):
    return offs[:16].T.reshape(-1).astype(np.int64)


def striped8(idx):
    return np.concatenate([x.reshape(-1, 16).T for x in idx]).astype(np.uint16)


def runs(offs, k):
    lists = np.stack([offs[16 * r : 16 * r + 16].T.reshape(-1) for r in range(8)]).astype(np.int64)
    return lists[np.arange(k) % 512 // 64]


def pack_weight(w):
    k, n = w.shape
    w = f64(np.asarray(w, np.float32).astype(ml_dtypes.bfloat16)).reshape(k // 32, 32, n)
    amax = np.abs(w).max(1)
    byte = np.clip(np.where(amax > 0, np.frexp(amax)[1] - 1 + 127 - 7, 1), 1, 254)
    scaled = (w * np.exp2(127.0 - byte)[:, None, :]).reshape(k, n).astype(np.float32)
    words = np.ascontiguousarray(scaled.reshape(k // 512, 128, 4, n).transpose(0, 1, 3, 2)).astype(ml_dtypes.float8_e4m3fn).view(np.uint8)
    return words, np.ascontiguousarray(byte.astype(np.uint8).reshape(k // 512, 16, n))


def unpack_weight(words, scales):
    g, p, n, _ = words.shape
    vals = np.ascontiguousarray(words).view(ml_dtypes.float8_e4m3fn).astype(np.float64) * np.repeat(np.exp2(scales.astype(np.float64) - 127.0), 8, axis=1)[..., None]
    return vals.transpose(0, 1, 3, 2).reshape(g * 512, n)


def sigmoid(v):
    return 1.0 / (1.0 + np.exp(-np.maximum(v, -700.0)))


K, T, S, N, H, J = 512, 2048, 256, 512, 512, 512


def setup_inputs():
    n = np.random.standard_normal
    s = mx_kscale(K)[:, None]
    u = mx_kscale(H)
    packed_xT = pack_weight(n((K, T)) * s)
    return {
        "x_words": packed_xT[0],
        "x_scales": packed_xT[1],
        "w1": (n((K, H)) / np.sqrt(K) / s).astype(np.float32),
        "gn": (np.random.uniform(0.5, 1.5, (H, 1)) * u[:, None]).astype(np.float32),
        "w2": (n((H, N)) / np.sqrt(H) / u[:, None]).astype(np.float32),
        "offs": striped(np.random.permutation(T)[:S]),
        "n1": striped(np.random.randint(0, S, J)),
        "n2": striped8(np.stack([np.random.permutation(S) for _ in range(8)])),
        "n3": striped8(np.stack([np.random.permutation(S) for _ in range(8)])),
        "n4": striped8(np.stack([np.random.permutation(S) for _ in range(8)])),
    }


def reference(x_words, x_scales, w1, gn, w2, offs, n1, n2, n3, n4):
    xq = unpack_weight(x_words, x_scales)[:, unstriped(offs)]
    y = mxq(f64(w1), 0, "e4m3").T @ xq
    mb = y[:, unstriped(n1)]
    mn = mb.reshape(H, S, 2).min(axis=2)
    mx = mb.reshape(H, S, 2).max(axis=2)
    z = f64(gn) * ((y - mn) * sigmoid(mx))
    h = mxq(f64(w2), 0, "e4m3").T @ mxq(z, 0, "e4m3")
    return np.maximum(h, h[np.arange(N)[:, None], runs(n2, N)]) - (np.maximum(h[np.arange(N)[:, None], runs(n3, N)], h[np.arange(N)[:, None], runs(n4, N)]))

@@ -1,0 +1,238 @@
+from contextlib import ExitStack
+
+import concourse.mybir as mybir
+
+K, T, S, N, H = 512, 2048, 256, 512, 512
+FLOPS = 2 * K * H * S + 2 * H * N * S
+
+F32 = mybir.dt.float32
+BF16 = mybir.dt.bfloat16
+I32 = mybir.dt.int32
+U32 = mybir.dt.uint32
+U16 = mybir.dt.uint16
+U8 = mybir.dt.uint8
+FP8X4 = mybir.dt.float8_e4m3fn_x4
+ALU = mybir.AluOpType
+COPY = mybir.ActivationFunctionType.Copy
+SIGMOID = mybir.ActivationFunctionType.Sigmoid
+
+P = 128
+PACK = 4
+HALF = S // 2
+Y_WINDOW = S + 16
+H_WINDOW = 2 * S
+W1_VECTOR_SHARE = 80
+
+
+def tile_picked_layghardmix_none_p_kernel(tc, x_words, x_scales, w1, gn, w2, offs, n1, n2, n3, n4, out):
+    nc = tc.nc
+    with ExitStack() as ctx:
+        keep = ctx.enter_context(tc.tile_pool(name="keep", bufs=1))
+        psum = ctx.enter_context(tc.psum_pool(name="psum", bufs=1))
+
+        def list_tile(name, src):
+            tile = keep.tile(list(src.shape), U16, name=name)
+            nc.sync.dma_start(tile[:], src)
+            return tile
+
+        scale_table = keep.tile([P, T], U8, name="scale_table")
+        nc.vector.memset(scale_table[:].bitcast(I32), 0)
+        w1_raw = keep.tile([P, PACK, H], F32, name="w1_raw")
+        nc.sync.dma_start(w1_raw[:], w1.rearrange("(p j) c -> p j c", j=PACK))
+        offs_sb = list_tile("offs_sb", offs)
+        word_table = keep.tile([P, T], I32, name="word_table")
+        nc.sync.dma_start(word_table[:], x_words[0].rearrange("p n t -> p (n t)").bitcast(I32))
+        n1_sb = list_tile("n1_sb", n1)
+        for q in range(4):
+            nc.scalar.dma_start(
+                scale_table[32 * q : 32 * q + 4, :].bitcast(I32),
+                x_scales[0, 4 * q : 4 * q + 4, :].bitcast(I32),
+            )
+        w2_raw = keep.tile([P, PACK, N], F32, name="w2_raw")
+        nc.sync.dma_start(w2_raw[:], w2.rearrange("(p j) c -> p j c", j=PACK))
+        gain = keep.tile([P, PACK], F32, name="gain")
+        nc.sync.dma_start(gain[:], gn.rearrange("(p t) o -> p (t o)", t=PACK))
+        n2_sb = list_tile("n2_sb", n2)
+        n3_sb = list_tile("n3_sb", n3)
+        n4_sb = list_tile("n4_sb", n4)
+
+        y_rows = [keep.tile([P, Y_WINDOW], F32, name=f"y_rows{t}") for t in range(PACK)]
+        h_rows = [keep.tile([P, H_WINDOW], F32, name=f"h_rows{t}") for t in range(PACK)]
+        for tile in y_rows + h_rows:
+            nc.gpsimd.memset(tile[:, S:], 0.0)
+
+        x_bytes = keep.tile([P, S], U8, name="x_bytes", align_bytes=64)
+        nc.vector.tensor_copy(x_bytes[:], scale_table[:].indirect(offs_sb[:]))
+
+        w1_bf = keep.tile([P, PACK, P, PACK], BF16, name="w1_bf", align_bytes=64)
+        w1_dst = w1_bf[:].rearrange("p t m j -> p m t j")
+        w1_src = w1_raw[:].rearrange("p j (m t) -> p m t j", t=PACK)
+        nc.vector.tensor_copy(w1_dst[:, :W1_VECTOR_SHARE], w1_src[:, :W1_VECTOR_SHARE])
+        nc.scalar.copy(w1_dst[:, W1_VECTOR_SHARE:], w1_src[:, W1_VECTOR_SHARE:])
+        w1_codes = keep.tile([P, H], U32, name="w1_codes", align_bytes=64)
+        w1_bytes = keep.tile([P, H], U8, name="w1_bytes", align_bytes=64)
+        nc.vector.quantize_mx(
+            out=w1_codes[:].bitcast(FP8X4), scales=w1_bytes[:], in_=w1_bf[:].rearrange("p t m j -> p (t m j)")
+        )
+
+        x_codes = keep.tile([P, S], U32, name="x_codes", align_bytes=64)
+        nc.vector.tensor_copy(x_codes[:], word_table[:].bitcast(U32).indirect(offs_sb[:]))
+
+        y_bank = [psum.tile([P, S], F32, name=f"y_bank{t}") for t in range(PACK)]
+        for t in range(PACK):
+            cols = slice(t * P, (t + 1) * P)
+            nc.tensor.matmul_mx(
+                out=y_bank[t][:],
+                lhsT=w1_codes[:, cols].bitcast(FP8X4),
+                lhsT_scale=w1_bytes[:, cols],
+                rhs=x_codes[:].bitcast(FP8X4),
+                rhs_scale=x_bytes[:],
+                start=True,
+                stop=True,
+            )
+        nc.scalar.copy(y_rows[0][:, :S], y_bank[0][:])
+        for t in range(1, PACK):
+            nc.vector.tensor_copy(y_rows[t][:, :S], y_bank[t][:])
+
+        w2_src = w2_raw[:].rearrange("p j (m t) -> p m t j", t=PACK)
+        w2_codes = {}
+        w2_bytes = [keep.tile([P, 2 * P], U8, name=f"w2_bytes{u}", align_bytes=64) for u in range(2)]
+
+        def round_w2(u, copy, tag):
+            tile = keep.tile([P, 2, P, PACK], BF16, name=f"w2_bf{u}", tag=tag, align_bytes=64)
+            copy(tile[:].rearrange("p t m j -> p m t j"), w2_src[:, :, 2 * u : 2 * u + 2, :])
+            return tile
+
+        def quantize_w2(u, tile, tag):
+            w2_codes[u] = keep.tile([P, 2 * P], U32, name=f"w2_codes{u}", tag=tag, align_bytes=64)
+            nc.vector.quantize_mx(
+                out=w2_codes[u][:].bitcast(FP8X4), scales=w2_bytes[u][:], in_=tile[:].rearrange("p t m j -> p (t m j)")
+            )
+
+        groups = {0: ((0, 1), (2, 3)), 1: ((0,), (1, 2), (3,))}
+        member_tag = {(1, 0): "larger0_0", (1, 1): "larger0_2"}
+        members = {}
+        larger = {}
+
+        def group_of(c, t):
+            return [g for g in groups[c] if t in g][0]
+
+        smaller = [keep.tile([P, PACK, HALF], F32, name=f"smaller{c}") for c in range(2)]
+        gate = [keep.tile([P, PACK, HALF], F32, name=f"gate{c}") for c in range(2)]
+        diff = [keep.tile([P, PACK, HALF], F32, name=f"diff{c}") for c in range(2)]
+        z_bf = [keep.tile([P, PACK, HALF], BF16, name=f"z_bf{c}") for c in range(2)]
+        z_words = [keep.tile([P, HALF, PACK], BF16, name=f"z_words{c}", tag=f"z_words{c}", align_bytes=64) for c in range(2)]
+        z_codes = [keep.tile([P, HALF], U32, name=f"z_codes{c}", align_bytes=64) for c in range(2)]
+        z_bytes = [keep.tile([P, HALF], U8, name=f"z_bytes{c}", align_bytes=64) for c in range(2)]
+
+        def fetch_members(c, t):
+            g = group_of(c, t)
+            if t == g[0]:
+                name = f"members{c}_{t}"
+                members[c, t] = keep.tile([P, len(g), S], F32, name=name, tag=member_tag.get((c, t), name), align_bytes=64)
+            nc.scalar.activation(members[c, g[0]][:, t - g[0], :], y_rows[t][:].indirect(n1_sb[:, 16 * c : 16 * (c + 1)]), COPY)
+
+        def extremes(c, g):
+            ts = slice(g[0], g[-1] + 1)
+            larger[c, g[0]] = keep.tile([P, len(g), HALF], F32, name=f"larger{c}_{g[0]}", tag=f"larger{c}_{g[0]}", align_bytes=64)
+            pair = members[c, g[0]][:].rearrange("p t (j e) -> p (t j) e", e=2)
+            nc.vector.tensor_tensor(larger[c, g[0]][:].rearrange("p t j -> p (t j)"), pair[:, :, 0], pair[:, :, 1], ALU.max)
+            nc.vector.tensor_tensor(smaller[c][:, ts, :].rearrange("p t j -> p (t j)"), pair[:, :, 0], pair[:, :, 1], ALU.min)
+
+        def differences(c, t):
+            nc.vector.tensor_tensor(diff[c][:, t, :], y_bank[t][:, c * HALF : (c + 1) * HALF], smaller[c][:, t, :], ALU.subtract)
+
+        def gates(c, g):
+            nc.scalar.activation(gate[c][:, g[0] : g[-1] + 1, :], larger[c, g[0]][:], SIGMOID)
+
+        def products(c, t):
+            nc.vector.scalar_tensor_tensor(z_bf[c][:, t, :], diff[c][:, t, :], gain[:, t : t + 1], gate[c][:, t, :], ALU.mult, ALU.mult)
+
+        def interleave_z(c):
+            nc.vector.tensor_copy(
+                z_words[c][:].rearrange("p (g i) t -> p g t i", i=4), z_bf[c][:].rearrange("p t (g i) -> p g t i", i=4)
+            )
+
+        def quantize_z(c):
+            nc.vector.quantize_mx(
+                out=z_codes[c][:].bitcast(FP8X4), scales=z_bytes[c][:], in_=z_words[c][:].rearrange("p j t -> p (j t)")
+            )
+
+        h_bank = [psum.tile([P, S], F32, name=f"h_bank{t}") for t in range(PACK)]
+
+        def second_product(c, t):
+            cols = slice((t % 2) * P, (t % 2 + 1) * P)
+            nc.tensor.matmul_mx(
+                out=h_bank[t][:, c * HALF : (c + 1) * HALF],
+                lhsT=w2_codes[t // 2][:, cols].bitcast(FP8X4),
+                lhsT_scale=w2_bytes[t // 2][:, cols],
+                rhs=z_codes[c][:].bitcast(FP8X4),
+                rhs_scale=z_bytes[c][:],
+                start=True,
+                stop=True,
+            )
+
+        fetch_members(0, 0)
+        fetch_members(0, 1)
+        extremes(0, (0, 1))
+        fetch_members(0, 2)
+        fetch_members(0, 3)
+        w2_early = round_w2(0, nc.vector.tensor_copy, "w2_bf0")
+        differences(0, 0)
+        differences(0, 1)
+        gates(0, (0, 1))
+        extremes(0, (2, 3))
+        quantize_w2(0, w2_early, "w2_codes0")
+        products(0, 0)
+        products(0, 1)
+        differences(0, 2)
+        differences(0, 3)
+        fetch_members(1, 0)
+        gates(0, (2, 3))
+        extremes(1, (0,))
+        products(0, 2)
+        products(0, 3)
+        differences(1, 0)
+        fetch_members(1, 1)
+        fetch_members(1, 2)
+        fetch_members(1, 3)
+        interleave_z(0)
+        gates(1, (0,))
+        extremes(1, (1, 2))
+        quantize_z(0)
+        second_product(0, 0)
+        second_product(0, 1)
+        gates(1, (1, 2))
+        extremes(1, (3,))
+        products(1, 0)
+        for t in range(1, PACK):
+            differences(1, t)
+        gates(1, (3,))
+        nc.scalar.copy(h_rows[0][:, :HALF], h_bank[0][:, :HALF])
+        for t in range(1, PACK):
+            products(1, t)
+        interleave_z(1)
+        w2_late = round_w2(1, nc.scalar.copy, "larger1_3")
+        quantize_z(1)
+        second_product(1, 0)
+        second_product(1, 1)
+        nc.scalar.copy(h_rows[0][:, HALF:S], h_bank[0][:, HALF:])
+        nc.vector.tensor_copy(h_rows[1][:, :S], h_bank[1][:])
+        quantize_w2(1, w2_late, "z_words1")
+        for t in range(2, PACK):
+            second_product(0, t)
+            second_product(1, t)
+            nc.vector.tensor_copy(h_rows[t][:, :S], h_bank[t][:])
+
+        out_rows = out.rearrange("(p t) j -> p t j", t=PACK)
+        for t in range(PACK):
+            fetched = keep.tile([P, 3, S], F32, name=f"fetched{t}")
+            for e, places in enumerate((n2_sb, n3_sb, n4_sb)):
+                nc.scalar.activation(fetched[:, e, :], h_rows[t][:].indirect(places[:]), COPY)
+            first = keep.tile([P, S], F32, name=f"first{t}")
+            second = keep.tile([P, S], F32, name=f"second{t}")
+            result = keep.tile([P, S], F32, name=f"result{t}")
+            nc.vector.tensor_tensor(first[:], fetched[:, 0, :], h_rows[t][:, :S], ALU.max)
+            nc.vector.tensor_tensor(second[:], fetched[:, 1, :], fetched[:, 2, :], ALU.max)
+            nc.vector.tensor_tensor(result[:], first[:], second[:], ALU.subtract)
+            nc.sync.dma_start(out_rows[:, t, :], result[:])

@@ -36,18 +36,22 @@ def tile_picked_layghardmix_none_p_kernel(tc, x_words, x_scales, w1, gn, w2, off
             return tile
 
         scale_table = keep.tile([P, T], U8, name="scale_table")
-        nc.vector.memset(scale_table[:].bitcast(I32), 0)
+        nc.gpsimd.memset(scale_table[:].bitcast(I32), 0)
+        warm = keep.tile([P, 8], F32, name="warm")
+        warm_out = keep.tile([P, 8], F32, name="warm_out")
+        nc.vector.memset(warm[:], 0.0)
+        nc.scalar.activation(warm_out[:], warm[:], SIGMOID)
         w1_raw = keep.tile([P, PACK, H], F32, name="w1_raw")
         nc.sync.dma_start(w1_raw[:], w1.rearrange("(p j) c -> p j c", j=PACK))
+        for q in range(4):
+            nc.sync.dma_start(
+                scale_table[32 * q : 32 * q + 4, :].bitcast(I32),
+                x_scales[0, 4 * q : 4 * q + 4, :].bitcast(I32),
+            )
         offs_sb = list_tile("offs_sb", offs)
         word_table = keep.tile([P, T], I32, name="word_table")
         nc.sync.dma_start(word_table[:], x_words[0].rearrange("p n t -> p (n t)").bitcast(I32))
         n1_sb = list_tile("n1_sb", n1)
-        for q in range(4):
-            nc.scalar.dma_start(
-                scale_table[32 * q : 32 * q + 4, :].bitcast(I32),
-                x_scales[0, 4 * q : 4 * q + 4, :].bitcast(I32),
-            )
         w2_raw = keep.tile([P, PACK, N], F32, name="w2_raw")
         nc.sync.dma_start(w2_raw[:], w2.rearrange("(p j) c -> p j c", j=PACK))
         gain = keep.tile([P, PACK], F32, name="gain")
@@ -59,7 +63,7 @@ def tile_picked_layghardmix_none_p_kernel(tc, x_words, x_scales, w1, gn, w2, off
         y_rows = [keep.tile([P, Y_WINDOW], F32, name=f"y_rows{t}") for t in range(PACK)]
         h_rows = [keep.tile([P, H_WINDOW], F32, name=f"h_rows{t}") for t in range(PACK)]
         for tile in y_rows + h_rows:
-            nc.gpsimd.memset(tile[:, S:], 0.0)
+            nc.vector.memset(tile[:, S:], 0.0)
 
         x_bytes = keep.tile([P, S], U8, name="x_bytes", align_bytes=64)
         nc.vector.tensor_copy(x_bytes[:], scale_table[:].indirect(offs_sb[:]))
@@ -78,7 +82,7 @@ def tile_picked_layghardmix_none_p_kernel(tc, x_words, x_scales, w1, gn, w2, off
         x_codes = keep.tile([P, S], U32, name="x_codes", align_bytes=64)
         nc.vector.tensor_copy(x_codes[:], word_table[:].bitcast(U32).indirect(offs_sb[:]))
 
-        y_bank = [psum.tile([P, S], F32, name=f"y_bank{t}") for t in range(PACK)]
+        y_bank = [psum.tile([P, S], F32, name=f"y_bank{t}", tag=f"y_bank{t}") for t in range(PACK)]
         for t in range(PACK):
             cols = slice(t * P, (t + 1) * P)
             nc.tensor.matmul_mx(
@@ -95,144 +99,164 @@ def tile_picked_layghardmix_none_p_kernel(tc, x_words, x_scales, w1, gn, w2, off
             nc.vector.tensor_copy(y_rows[t][:, :S], y_bank[t][:])
 
         w2_src = w2_raw[:].rearrange("p j (m t) -> p m t j", t=PACK)
-        w2_codes = {}
-        w2_bytes = [keep.tile([P, 2 * P], U8, name=f"w2_bytes{u}", align_bytes=64) for u in range(2)]
+        w2_codes = keep.tile([P, N], U32, name="w2_codes", align_bytes=64)
+        w2_bytes = keep.tile([P, N], U8, name="w2_bytes", align_bytes=64)
 
-        def round_w2(u, copy, tag):
-            tile = keep.tile([P, 2, P, PACK], BF16, name=f"w2_bf{u}", tag=tag, align_bytes=64)
-            copy(tile[:].rearrange("p t m j -> p m t j"), w2_src[:, :, 2 * u : 2 * u + 2, :])
-            return tile
-
-        def quantize_w2(u, tile, tag):
-            w2_codes[u] = keep.tile([P, 2 * P], U32, name=f"w2_codes{u}", tag=tag, align_bytes=64)
-            nc.vector.quantize_mx(
-                out=w2_codes[u][:].bitcast(FP8X4), scales=w2_bytes[u][:], in_=tile[:].rearrange("p t m j -> p (t m j)")
+        def round_w2(tile, first, t0, t1):
+            nc.vector.tensor_copy(
+                tile[:, t0 - first : t1 - first].rearrange("p t m j -> p m t j"), w2_src[:, :, t0:t1, :]
             )
 
-        groups = {0: ((0, 1), (2, 3)), 1: ((0,), (1, 2), (3,))}
-        member_tag = {(1, 0): "larger0_0", (1, 1): "larger0_2"}
-        members = {}
-        larger = {}
-
-        def group_of(c, t):
-            return [g for g in groups[c] if t in g][0]
+        def quantize_w2(tile, first, t0, t1):
+            nc.vector.quantize_mx(
+                out=w2_codes[:, t0 * P : t1 * P].bitcast(FP8X4),
+                scales=w2_bytes[:, t0 * P : t1 * P],
+                in_=tile[:, t0 - first : t1 - first].rearrange("p t m j -> p (t m j)"),
+            )
 
         smaller = [keep.tile([P, PACK, HALF], F32, name=f"smaller{c}") for c in range(2)]
         gate = [keep.tile([P, PACK, HALF], F32, name=f"gate{c}") for c in range(2)]
         diff = [keep.tile([P, PACK, HALF], F32, name=f"diff{c}") for c in range(2)]
         z_bf = [keep.tile([P, PACK, HALF], BF16, name=f"z_bf{c}") for c in range(2)]
-        z_words = [keep.tile([P, HALF, PACK], BF16, name=f"z_words{c}", tag=f"z_words{c}", align_bytes=64) for c in range(2)]
-        z_codes = [keep.tile([P, HALF], U32, name=f"z_codes{c}", align_bytes=64) for c in range(2)]
-        z_bytes = [keep.tile([P, HALF], U8, name=f"z_bytes{c}", align_bytes=64) for c in range(2)]
+        z_codes = keep.tile([P, S], U32, name="z_codes", align_bytes=64)
+        z_bytes = keep.tile([P, S], U8, name="z_bytes", align_bytes=64)
+        members = {}
+        larger = {}
+        z_words = {}
+
+        def member_tile(c, t0, t1, tag):
+            tile = keep.tile([P, t1 - t0, S], F32, name=f"members{c}_{t0}", tag=tag, align_bytes=64)
+            for t in range(t0, t1):
+                members[c, t] = (tile, t0)
 
         def fetch_members(c, t):
-            g = group_of(c, t)
-            if t == g[0]:
-                name = f"members{c}_{t}"
-                members[c, t] = keep.tile([P, len(g), S], F32, name=name, tag=member_tag.get((c, t), name), align_bytes=64)
-            nc.scalar.activation(members[c, g[0]][:, t - g[0], :], y_rows[t][:].indirect(n1_sb[:, 16 * c : 16 * (c + 1)]), COPY)
+            tile, first = members[c, t]
+            nc.scalar.activation(tile[:, t - first, :], y_rows[t][:].indirect(n1_sb[:, 16 * c : 16 * (c + 1)]), COPY)
 
-        def extremes(c, g):
-            ts = slice(g[0], g[-1] + 1)
-            larger[c, g[0]] = keep.tile([P, len(g), HALF], F32, name=f"larger{c}_{g[0]}", tag=f"larger{c}_{g[0]}", align_bytes=64)
-            pair = members[c, g[0]][:].rearrange("p t (j e) -> p (t j) e", e=2)
-            nc.vector.tensor_tensor(larger[c, g[0]][:].rearrange("p t j -> p (t j)"), pair[:, :, 0], pair[:, :, 1], ALU.max)
-            nc.vector.tensor_tensor(smaller[c][:, ts, :].rearrange("p t j -> p (t j)"), pair[:, :, 0], pair[:, :, 1], ALU.min)
+        def maxima(c, t0, t1):
+            larger[c, t0] = keep.tile([P, t1 - t0, HALF], F32, name=f"larger{c}_{t0}", tag=f"larger{c}_{t0}", align_bytes=64)
+            extreme(c, t0, t1, larger[c, t0][:], ALU.max)
 
-        def differences(c, t):
+        def minima(c, t0, t1):
+            extreme(c, t0, t1, smaller[c][:, t0:t1, :], ALU.min)
+
+        def extreme(c, t0, t1, dst, op):
+            tile, first = members[c, t0]
+            pair = tile[:, t0 - first : t1 - first, :].rearrange("p t (j e) -> p t j e", e=2)
+            nc.vector.tensor_tensor(dst, pair[:, :, :, 0], pair[:, :, :, 1], op)
+
+        def difference(c, t):
             nc.vector.tensor_tensor(diff[c][:, t, :], y_bank[t][:, c * HALF : (c + 1) * HALF], smaller[c][:, t, :], ALU.subtract)
 
-        def gates(c, g):
-            nc.scalar.activation(gate[c][:, g[0] : g[-1] + 1, :], larger[c, g[0]][:], SIGMOID)
+        def gates(c, t0, t1):
+            nc.scalar.activation(gate[c][:, t0:t1, :], larger[c, t0][:], SIGMOID)
 
-        def products(c, t):
+        def product(c, t):
             nc.vector.scalar_tensor_tensor(z_bf[c][:, t, :], diff[c][:, t, :], gain[:, t : t + 1], gate[c][:, t, :], ALU.mult, ALU.mult)
 
-        def interleave_z(c):
-            nc.vector.tensor_copy(
-                z_words[c][:].rearrange("p (g i) t -> p g t i", i=4), z_bf[c][:].rearrange("p t (g i) -> p g t i", i=4)
-            )
+        def interleave_z(c, copy, tag):
+            z_words[c] = keep.tile([P, HALF, PACK], BF16, name=f"z_words{c}", tag=tag, align_bytes=64)
+            copy(z_words[c][:].rearrange("p (g i) t -> p g t i", i=4), z_bf[c][:].rearrange("p t (g i) -> p g t i", i=4))
 
         def quantize_z(c):
+            cols = slice(c * HALF, (c + 1) * HALF)
             nc.vector.quantize_mx(
-                out=z_codes[c][:].bitcast(FP8X4), scales=z_bytes[c][:], in_=z_words[c][:].rearrange("p j t -> p (j t)")
+                out=z_codes[:, cols].bitcast(FP8X4), scales=z_bytes[:, cols], in_=z_words[c][:].rearrange("p j t -> p (j t)")
             )
 
-        h_bank = [psum.tile([P, S], F32, name=f"h_bank{t}") for t in range(PACK)]
-
-        def second_product(c, t):
-            cols = slice((t % 2) * P, (t % 2 + 1) * P)
+        def second_product(t, cols, tag):
+            bank = psum.tile([P, cols.stop - cols.start], F32, name=f"h_bank{t}_{cols.start}", tag=tag)
+            rows = slice(t * P, (t + 1) * P)
             nc.tensor.matmul_mx(
-                out=h_bank[t][:, c * HALF : (c + 1) * HALF],
-                lhsT=w2_codes[t // 2][:, cols].bitcast(FP8X4),
-                lhsT_scale=w2_bytes[t // 2][:, cols],
-                rhs=z_codes[c][:].bitcast(FP8X4),
-                rhs_scale=z_bytes[c][:],
+                out=bank[:],
+                lhsT=w2_codes[:, rows].bitcast(FP8X4),
+                lhsT_scale=w2_bytes[:, rows],
+                rhs=z_codes[:, cols].bitcast(FP8X4),
+                rhs_scale=z_bytes[:, cols],
                 start=True,
                 stop=True,
             )
+            return bank
 
-        fetch_members(0, 0)
-        fetch_members(0, 1)
-        extremes(0, (0, 1))
-        fetch_members(0, 2)
-        fetch_members(0, 3)
-        w2_early = round_w2(0, nc.vector.tensor_copy, "w2_bf0")
-        differences(0, 0)
-        differences(0, 1)
-        gates(0, (0, 1))
-        extremes(0, (2, 3))
-        quantize_w2(0, w2_early, "w2_codes0")
-        products(0, 0)
-        products(0, 1)
-        differences(0, 2)
-        differences(0, 3)
+        member_tile(0, 0, PACK, "members0")
+        for t in range(PACK):
+            fetch_members(0, t)
+        w2_first = keep.tile([P, 1, P, PACK], BF16, name="w2_first", align_bytes=64)
+        round_w2(w2_first, 0, 0, 1)
+        maxima(0, 0, 2)
+        minima(0, 0, 2)
+        gates(0, 0, 2)
+        quantize_w2(w2_first, 0, 0, 1)
+        difference(0, 0)
+        difference(0, 1)
+        maxima(0, 2, 4)
+        minima(0, 2, 4)
+        member_tile(1, 0, 1, "larger0_0")
         fetch_members(1, 0)
-        gates(0, (2, 3))
-        extremes(1, (0,))
-        products(0, 2)
-        products(0, 3)
-        differences(1, 0)
+        gates(0, 2, 4)
+        member_tile(1, 1, 3, "larger0_2")
         fetch_members(1, 1)
         fetch_members(1, 2)
+        product(0, 0)
+        product(0, 1)
+        difference(0, 2)
+        difference(0, 3)
+        product(0, 2)
+        product(0, 3)
+        maxima(1, 0, 1)
+        minima(1, 0, 1)
+        maxima(1, 1, 2)
+        minima(1, 1, 2)
+        gates(1, 0, 1)
+        gates(1, 1, 2)
+        member_tile(1, 3, 4, "larger1_1")
         fetch_members(1, 3)
-        interleave_z(0)
-        gates(1, (0,))
-        extremes(1, (1, 2))
+        difference(1, 0)
+        maxima(1, 2, 3)
+        difference(1, 1)
+        minima(1, 2, 3)
+        gates(1, 2, 3)
+        product(1, 0)
+        product(1, 1)
+        maxima(1, 3, 4)
+        minima(1, 3, 4)
+        gates(1, 3, 4)
+        interleave_z(0, nc.scalar.copy, "larger1_3")
+        difference(1, 2)
+        difference(1, 3)
+        product(1, 2)
+        product(1, 3)
         quantize_z(0)
-        second_product(0, 0)
-        second_product(0, 1)
-        gates(1, (1, 2))
-        extremes(1, (3,))
-        products(1, 0)
-        for t in range(1, PACK):
-            differences(1, t)
-        gates(1, (3,))
-        nc.scalar.copy(h_rows[0][:, :HALF], h_bank[0][:, :HALF])
-        for t in range(1, PACK):
-            products(1, t)
-        interleave_z(1)
-        w2_late = round_w2(1, nc.scalar.copy, "larger1_3")
+        interleave_z(1, nc.vector.tensor_copy, "z_words1")
+        bank = second_product(0, slice(0, HALF), "h_bank_a")
+        nc.scalar.copy(h_rows[0][:, :HALF], bank[:])
         quantize_z(1)
-        second_product(1, 0)
-        second_product(1, 1)
-        nc.scalar.copy(h_rows[0][:, HALF:S], h_bank[0][:, HALF:])
-        nc.vector.tensor_copy(h_rows[1][:, :S], h_bank[1][:])
-        quantize_w2(1, w2_late, "z_words1")
-        for t in range(2, PACK):
-            second_product(0, t)
-            second_product(1, t)
-            nc.vector.tensor_copy(h_rows[t][:, :S], h_bank[t][:])
+        bank = second_product(0, slice(HALF, S), "h_bank_b")
+        nc.scalar.copy(h_rows[0][:, HALF:S], bank[:])
+        w2_rest = keep.tile([P, PACK - 1, P, PACK], BF16, name="w2_rest", tag="z_words1", align_bytes=64)
+        round_w2(w2_rest, 1, 1, 2)
+        round_w2(w2_rest, 1, 2, PACK)
+        quantize_w2(w2_rest, 1, 1, 2)
+        quantize_w2(w2_rest, 1, 2, PACK)
+        for t in range(1, PACK):
+            bank = second_product(t, slice(0, S), f"y_bank{t}")
+            nc.vector.tensor_copy(h_rows[t][:, :S], bank[:])
 
         out_rows = out.rearrange("(p t) j -> p t j", t=PACK)
         for t in range(PACK):
             fetched = keep.tile([P, 3, S], F32, name=f"fetched{t}")
-            for e, places in enumerate((n2_sb, n3_sb, n4_sb)):
-                nc.scalar.activation(fetched[:, e, :], h_rows[t][:].indirect(places[:]), COPY)
             first = keep.tile([P, S], F32, name=f"first{t}")
             second = keep.tile([P, S], F32, name=f"second{t}")
             result = keep.tile([P, S], F32, name=f"result{t}")
+            nc.scalar.activation(fetched[:, 0, :], h_rows[t][:].indirect(n2_sb[:]), COPY)
+            nc.scalar.activation(fetched[:, 1, :], h_rows[t][:].indirect(n3_sb[:]), COPY)
             nc.vector.tensor_tensor(first[:], fetched[:, 0, :], h_rows[t][:, :S], ALU.max)
-            nc.vector.tensor_tensor(second[:], fetched[:, 1, :], fetched[:, 2, :], ALU.max)
-            nc.vector.tensor_tensor(result[:], first[:], second[:], ALU.subtract)
-            nc.sync.dma_start(out_rows[:, t, :], result[:])
+            pieces = 2 if t == PACK - 1 else 1
+            width = S // pieces
+            for piece in range(pieces):
+                cols = slice(piece * width, (piece + 1) * width)
+                places = n4_sb[:, cols.start // 16 : cols.stop // 16]
+                nc.scalar.activation(fetched[:, 2, cols], h_rows[t][:].indirect(places), COPY)
+                nc.vector.tensor_tensor(second[:, cols], fetched[:, 1, cols], fetched[:, 2, cols], ALU.max)
+                nc.vector.tensor_tensor(result[:, cols], first[:, cols], second[:, cols], ALU.subtract)
+                nc.sync.dma_start(out_rows[:, t, cols], result[:, cols])

@@ -19,7 +19,7 @@ SIGMOID = mybir.ActivationFunctionType.Sigmoid
 P = 128
 PACK = 4
 HALF = S // 2
-Y_WINDOW = S + 16
+Y_WINDOW = 2 * S + 16
 H_WINDOW = 2 * S
 W1_VECTOR_SHARE = 80
 
@@ -82,21 +82,25 @@ def tile_picked_layghardmix_none_p_kernel(tc, x_words, x_scales, w1, gn, w2, off
         x_codes = keep.tile([P, S], U32, name="x_codes", align_bytes=64)
         nc.vector.tensor_copy(x_codes[:], word_table[:].bitcast(U32).indirect(offs_sb[:]))
 
-        y_bank = [psum.tile([P, S], F32, name=f"y_bank{t}", tag=f"y_bank{t}") for t in range(PACK)]
-        for t in range(PACK):
-            cols = slice(t * P, (t + 1) * P)
+        def first_product(t, cols, tag):
+            bank = psum.tile([P, cols.stop - cols.start], F32, name=f"y_bank{t}_{cols.start}", tag=tag)
+            rows = slice(t * P, (t + 1) * P)
             nc.tensor.matmul_mx(
-                out=y_bank[t][:],
-                lhsT=w1_codes[:, cols].bitcast(FP8X4),
-                lhsT_scale=w1_bytes[:, cols],
-                rhs=x_codes[:].bitcast(FP8X4),
-                rhs_scale=x_bytes[:],
+                out=bank[:],
+                lhsT=w1_codes[:, rows].bitcast(FP8X4),
+                lhsT_scale=w1_bytes[:, rows],
+                rhs=x_codes[:, cols].bitcast(FP8X4),
+                rhs_scale=x_bytes[:, cols],
                 start=True,
                 stop=True,
             )
-        nc.scalar.copy(y_rows[0][:, :S], y_bank[0][:])
-        for t in range(1, PACK):
-            nc.vector.tensor_copy(y_rows[t][:, :S], y_bank[t][:])
+            return bank
+
+        nc.scalar.copy(y_rows[0][:, :HALF], first_product(0, slice(0, HALF), "half_bank0")[:])
+        nc.vector.tensor_copy(y_rows[0][:, HALF:S], first_product(0, slice(HALF, S), "half_bank1")[:])
+        for t in range(1, PACK - 1):
+            nc.vector.tensor_copy(y_rows[t][:, :S], first_product(t, slice(0, S), f"bank{t}")[:])
+        last_bank = first_product(PACK - 1, slice(0, S), f"bank{PACK - 1}")
 
         w2_src = w2_raw[:].rearrange("p j (m t) -> p m t j", t=PACK)
         w2_codes = keep.tile([P, N], U32, name="w2_codes", align_bytes=64)
@@ -114,49 +118,52 @@ def tile_picked_layghardmix_none_p_kernel(tc, x_words, x_scales, w1, gn, w2, off
                 in_=tile[:, t0 - first : t1 - first].rearrange("p t m j -> p (t m j)"),
             )
 
-        smaller = [keep.tile([P, PACK, HALF], F32, name=f"smaller{c}") for c in range(2)]
-        gate = [keep.tile([P, PACK, HALF], F32, name=f"gate{c}") for c in range(2)]
-        diff = [keep.tile([P, PACK, HALF], F32, name=f"diff{c}") for c in range(2)]
-        z_bf = [keep.tile([P, PACK, HALF], BF16, name=f"z_bf{c}") for c in range(2)]
+        pieces = [(0, 0, S), (1, 0, S), (2, 0, S), (3, 0, S)]
+        z_bf = keep.tile([P, 2, PACK, HALF], BF16, name="z_bf")
         z_codes = keep.tile([P, S], U32, name="z_codes", align_bytes=64)
         z_bytes = keep.tile([P, S], U8, name="z_bytes", align_bytes=64)
-        members = {}
-        larger = {}
-        z_words = {}
+        members, larger, smaller, gate, diff, z_words = {}, {}, {}, {}, {}, {}
 
-        def member_tile(c, t0, t1, tag):
-            tile = keep.tile([P, t1 - t0, S], F32, name=f"members{c}_{t0}", tag=tag, align_bytes=64)
-            for t in range(t0, t1):
-                members[c, t] = (tile, t0)
+        def piece_tile(kind, n, factor=1, tag=None):
+            t, lo, hi = pieces[n]
+            return keep.tile([P, factor * (hi - lo)], F32, name=f"{kind}{n}", tag=tag or f"{kind}{n}", align_bytes=64)
 
-        def fetch_members(c, t):
-            tile, first = members[c, t]
-            nc.scalar.activation(tile[:, t - first, :], y_rows[t][:].indirect(n1_sb[:, 16 * c : 16 * (c + 1)]), COPY)
+        def fetch_members(n, tag=None):
+            t, lo, hi = pieces[n]
+            members[n] = piece_tile("members", n, 2, tag)
+            nc.scalar.activation(members[n][:], y_rows[t][:].indirect(n1_sb[:, lo // 8 : hi // 8]), COPY)
 
-        def maxima(c, t0, t1):
-            larger[c, t0] = keep.tile([P, t1 - t0, HALF], F32, name=f"larger{c}_{t0}", tag=f"larger{c}_{t0}", align_bytes=64)
-            extreme(c, t0, t1, larger[c, t0][:], ALU.max)
+        def maximum(n):
+            larger[n] = piece_tile("larger", n)
+            nc.vector.tensor_tensor(larger[n][:], members[n][:, 0::2], members[n][:, 1::2], ALU.max)
 
-        def minima(c, t0, t1):
-            extreme(c, t0, t1, smaller[c][:, t0:t1, :], ALU.min)
+        def minimum(n):
+            smaller[n] = piece_tile("smaller", n)
+            nc.vector.tensor_tensor(smaller[n][:], members[n][:, 0::2], members[n][:, 1::2], ALU.min)
 
-        def extreme(c, t0, t1, dst, op):
-            tile, first = members[c, t0]
-            pair = tile[:, t0 - first : t1 - first, :].rearrange("p t (j e) -> p t j e", e=2)
-            nc.vector.tensor_tensor(dst, pair[:, :, :, 0], pair[:, :, :, 1], op)
+        def difference(n):
+            t, lo, hi = pieces[n]
+            diff[n] = piece_tile("diff", n)
+            nc.vector.tensor_tensor(diff[n][:], y_rows[t][:, lo:hi], smaller[n][:], ALU.subtract)
 
-        def difference(c, t):
-            nc.vector.tensor_tensor(diff[c][:, t, :], y_bank[t][:, c * HALF : (c + 1) * HALF], smaller[c][:, t, :], ALU.subtract)
+        def sigmoid(n):
+            gate[n] = piece_tile("gate", n)
+            nc.scalar.activation(gate[n][:], larger[n][:], SIGMOID)
 
-        def gates(c, t0, t1):
-            nc.scalar.activation(gate[c][:, t0:t1, :], larger[c, t0][:], SIGMOID)
-
-        def product(c, t):
-            nc.vector.scalar_tensor_tensor(z_bf[c][:, t, :], diff[c][:, t, :], gain[:, t : t + 1], gate[c][:, t, :], ALU.mult, ALU.mult)
+        def product(n, lo=0, hi=S):
+            t = n
+            nc.vector.scalar_tensor_tensor(
+                z_bf[:, lo // HALF : hi // HALF, t, :],
+                diff[n][:, lo:hi].rearrange("p (c j) -> p c j", j=HALF),
+                gain[:, t : t + 1],
+                gate[n][:, lo:hi].rearrange("p (c j) -> p c j", j=HALF),
+                ALU.mult,
+                ALU.mult,
+            )
 
         def interleave_z(c, copy, tag):
             z_words[c] = keep.tile([P, HALF, PACK], BF16, name=f"z_words{c}", tag=tag, align_bytes=64)
-            copy(z_words[c][:].rearrange("p (g i) t -> p g t i", i=4), z_bf[c][:].rearrange("p t (g i) -> p g t i", i=4))
+            copy(z_words[c][:].rearrange("p (g i) t -> p g t i", i=4), z_bf[:, c].rearrange("p t (g i) -> p g t i", i=4))
 
         def quantize_z(c):
             cols = slice(c * HALF, (c + 1) * HALF)
@@ -178,68 +185,50 @@ def tile_picked_layghardmix_none_p_kernel(tc, x_words, x_scales, w1, gn, w2, off
             )
             return bank
 
-        member_tile(0, 0, PACK, "members0")
-        for t in range(PACK):
-            fetch_members(0, t)
+        fetch_members(0)
+        fetch_members(1)
         w2_first = keep.tile([P, 1, P, PACK], BF16, name="w2_first", align_bytes=64)
         round_w2(w2_first, 0, 0, 1)
-        maxima(0, 0, 2)
-        minima(0, 0, 2)
-        gates(0, 0, 2)
+        maximum(0)
+        minimum(0)
         quantize_w2(w2_first, 0, 0, 1)
-        difference(0, 0)
-        difference(0, 1)
-        maxima(0, 2, 4)
-        minima(0, 2, 4)
-        member_tile(1, 0, 1, "larger0_0")
-        fetch_members(1, 0)
-        gates(0, 2, 4)
-        member_tile(1, 1, 3, "larger0_2")
-        fetch_members(1, 1)
-        fetch_members(1, 2)
-        product(0, 0)
-        product(0, 1)
-        difference(0, 2)
-        difference(0, 3)
-        product(0, 2)
-        product(0, 3)
-        maxima(1, 0, 1)
-        minima(1, 0, 1)
-        maxima(1, 1, 2)
-        minima(1, 1, 2)
-        gates(1, 0, 1)
-        gates(1, 1, 2)
-        member_tile(1, 3, 4, "larger1_1")
-        fetch_members(1, 3)
-        difference(1, 0)
-        maxima(1, 2, 3)
-        difference(1, 1)
-        minima(1, 2, 3)
-        gates(1, 2, 3)
-        product(1, 0)
-        product(1, 1)
-        maxima(1, 3, 4)
-        minima(1, 3, 4)
-        gates(1, 3, 4)
-        interleave_z(0, nc.scalar.copy, "larger1_3")
-        difference(1, 2)
-        difference(1, 3)
-        product(1, 2)
-        product(1, 3)
+        difference(0)
+        sigmoid(0)
+        fetch_members(2, "members0")
+        maximum(1)
+        minimum(1)
+        product(0)
+        difference(1)
+        sigmoid(1)
+        nc.scalar.copy(y_rows[PACK - 1][:, :S], last_bank[:])
+        fetch_members(3, "members1")
+        maximum(2)
+        minimum(2)
+        product(1)
+        difference(2)
+        sigmoid(2)
+        minimum(3)
+        maximum(3)
+        sigmoid(3)
+        difference(3)
+        product(2)
+        product(3, 0, HALF)
+        product(3, HALF, S)
+        interleave_z(0, nc.vector.tensor_copy, "z_words0")
+        interleave_z(1, nc.scalar.copy, "z_words1")
         quantize_z(0)
-        interleave_z(1, nc.vector.tensor_copy, "z_words1")
-        bank = second_product(0, slice(0, HALF), "h_bank_a")
+        bank = second_product(0, slice(0, HALF), "half_bank0")
         nc.scalar.copy(h_rows[0][:, :HALF], bank[:])
         quantize_z(1)
-        bank = second_product(0, slice(HALF, S), "h_bank_b")
+        bank = second_product(0, slice(HALF, S), "half_bank1")
         nc.scalar.copy(h_rows[0][:, HALF:S], bank[:])
         w2_rest = keep.tile([P, PACK - 1, P, PACK], BF16, name="w2_rest", tag="z_words1", align_bytes=64)
         round_w2(w2_rest, 1, 1, 2)
-        round_w2(w2_rest, 1, 2, PACK)
-        quantize_w2(w2_rest, 1, 1, 2)
-        quantize_w2(w2_rest, 1, 2, PACK)
         for t in range(1, PACK):
-            bank = second_product(t, slice(0, S), f"y_bank{t}")
+            if t + 1 < PACK:
+                round_w2(w2_rest, 1, t + 1, t + 2)
+            quantize_w2(w2_rest, 1, t, t + 1)
+            bank = second_product(t, slice(0, S), f"bank{t}")
             nc.vector.tensor_copy(h_rows[t][:, :S], bank[:])
 
         out_rows = out.rearrange("(p t) j -> p t j", t=PACK)
@@ -251,9 +240,9 @@ def tile_picked_layghardmix_none_p_kernel(tc, x_words, x_scales, w1, gn, w2, off
             nc.scalar.activation(fetched[:, 0, :], h_rows[t][:].indirect(n2_sb[:]), COPY)
             nc.scalar.activation(fetched[:, 1, :], h_rows[t][:].indirect(n3_sb[:]), COPY)
             nc.vector.tensor_tensor(first[:], fetched[:, 0, :], h_rows[t][:, :S], ALU.max)
-            pieces = 2 if t == PACK - 1 else 1
-            width = S // pieces
-            for piece in range(pieces):
+            parts = 2 if t == PACK - 1 else 1
+            width = S // parts
+            for piece in range(parts):
                 cols = slice(piece * width, (piece + 1) * width)
                 places = n4_sb[:, cols.start // 16 : cols.stop // 16]
                 nc.scalar.activation(fetched[:, 2, cols], h_rows[t][:].indirect(places), COPY)

@@ -98,9 +98,8 @@ def tile_picked_layghardmix_none_p_kernel(tc, x_words, x_scales, w1, gn, w2, off
 
         nc.scalar.copy(y_rows[0][:, :HALF], first_product(0, slice(0, HALF), "half_bank0")[:])
         nc.vector.tensor_copy(y_rows[0][:, HALF:S], first_product(0, slice(HALF, S), "half_bank1")[:])
-        for t in range(1, PACK - 1):
+        for t in range(1, PACK):
             nc.vector.tensor_copy(y_rows[t][:, :S], first_product(t, slice(0, S), f"bank{t}")[:])
-        last_bank = first_product(PACK - 1, slice(0, S), f"bank{PACK - 1}")
 
         w2_src = w2_raw[:].rearrange("p j (m t) -> p m t j", t=PACK)
         w2_codes = keep.tile([P, N], U32, name="w2_codes", align_bytes=64)
@@ -200,7 +199,6 @@ def tile_picked_layghardmix_none_p_kernel(tc, x_words, x_scales, w1, gn, w2, off
         product(0)
         difference(1)
         sigmoid(1)
-        nc.scalar.copy(y_rows[PACK - 1][:, :S], last_bank[:])
         fetch_members(3, "members1")
         maximum(2)
         minimum(2)
@@ -246,6 +244,9 @@ def tile_picked_layghardmix_none_p_kernel(tc, x_words, x_scales, w1, gn, w2, off
                 cols = slice(piece * width, (piece + 1) * width)
                 places = n4_sb[:, cols.start // 16 : cols.stop // 16]
                 nc.scalar.activation(fetched[:, 2, cols], h_rows[t][:].indirect(places), COPY)
-                nc.vector.tensor_tensor(second[:, cols], fetched[:, 1, cols], fetched[:, 2, cols], ALU.max)
-                nc.vector.tensor_tensor(result[:, cols], first[:, cols], second[:, cols], ALU.subtract)
+                runs = [slice(cols.start + r * width // parts, cols.start + (r + 1) * width // parts) for r in range(parts)]
+                for run in runs:
+                    nc.vector.tensor_tensor(second[:, run], fetched[:, 1, run], fetched[:, 2, run], ALU.max)
+                for run in runs:
+                    nc.vector.tensor_tensor(result[:, run], first[:, run], second[:, run], ALU.subtract)
                 nc.sync.dma_start(out_rows[:, t, cols], result[:, cols])

from contextlib import ExitStack

import concourse.mybir as mybir

K, T, S, N, H = 512, 2048, 256, 512, 512
FLOPS = 2 * K * H * S + 2 * H * N * S

F32 = mybir.dt.float32
BF16 = mybir.dt.bfloat16
I32 = mybir.dt.int32
U32 = mybir.dt.uint32
U16 = mybir.dt.uint16
U8 = mybir.dt.uint8
FP8X4 = mybir.dt.float8_e4m3fn_x4
ALU = mybir.AluOpType
COPY = mybir.ActivationFunctionType.Copy
SIGMOID = mybir.ActivationFunctionType.Sigmoid

P = 128
PACK = 4
HALF = S // 2
Y_WINDOW = 2 * S + 16
H_WINDOW = 2 * S
W1_VECTOR_SHARE = 80


def tile_picked_layghardmix_none_p_kernel(tc, x_words, x_scales, w1, gn, w2, offs, n1, n2, n3, n4, out):
    nc = tc.nc
    with ExitStack() as ctx:
        keep = ctx.enter_context(tc.tile_pool(name="keep", bufs=1))
        psum = ctx.enter_context(tc.psum_pool(name="psum", bufs=1))

        def list_tile(name, src):
            tile = keep.tile(list(src.shape), U16, name=name)
            nc.sync.dma_start(tile[:], src)
            return tile

        scale_table = keep.tile([P, T], U8, name="scale_table")
        nc.gpsimd.memset(scale_table[:].bitcast(I32), 0)
        warm = keep.tile([P, 8], F32, name="warm")
        warm_out = keep.tile([P, 8], F32, name="warm_out")
        nc.vector.memset(warm[:], 0.0)
        nc.scalar.activation(warm_out[:], warm[:], SIGMOID)
        w1_raw = keep.tile([P, PACK, H], F32, name="w1_raw")
        nc.sync.dma_start(w1_raw[:], w1.rearrange("(p j) c -> p j c", j=PACK))
        for q in range(4):
            nc.sync.dma_start(
                scale_table[32 * q : 32 * q + 4, :].bitcast(I32),
                x_scales[0, 4 * q : 4 * q + 4, :].bitcast(I32),
            )
        offs_sb = list_tile("offs_sb", offs)
        word_table = keep.tile([P, T], I32, name="word_table")
        nc.sync.dma_start(word_table[:], x_words[0].rearrange("p n t -> p (n t)").bitcast(I32))
        n1_sb = list_tile("n1_sb", n1)
        w2_raw = keep.tile([P, PACK, N], F32, name="w2_raw")
        nc.sync.dma_start(w2_raw[:], w2.rearrange("(p j) c -> p j c", j=PACK))
        gain = keep.tile([P, PACK], F32, name="gain")
        nc.sync.dma_start(gain[:], gn.rearrange("(p t) o -> p (t o)", t=PACK))
        n2_sb = list_tile("n2_sb", n2)
        n3_sb = list_tile("n3_sb", n3)
        n4_sb = list_tile("n4_sb", n4)

        y_rows = [keep.tile([P, Y_WINDOW], F32, name=f"y_rows{t}") for t in range(PACK)]
        h_rows = [keep.tile([P, H_WINDOW], F32, name=f"h_rows{t}") for t in range(PACK)]
        for tile in y_rows + h_rows:
            nc.vector.memset(tile[:, S:], 0.0)

        x_bytes = keep.tile([P, S], U8, name="x_bytes", align_bytes=64)
        nc.vector.tensor_copy(x_bytes[:], scale_table[:].indirect(offs_sb[:]))

        w1_bf = keep.tile([P, PACK, P, PACK], BF16, name="w1_bf", align_bytes=64)
        w1_dst = w1_bf[:].rearrange("p t m j -> p m t j")
        w1_src = w1_raw[:].rearrange("p j (m t) -> p m t j", t=PACK)
        nc.vector.tensor_copy(w1_dst[:, :W1_VECTOR_SHARE], w1_src[:, :W1_VECTOR_SHARE])
        nc.scalar.copy(w1_dst[:, W1_VECTOR_SHARE:], w1_src[:, W1_VECTOR_SHARE:])
        w1_codes = keep.tile([P, H], U32, name="w1_codes", align_bytes=64)
        w1_bytes = keep.tile([P, H], U8, name="w1_bytes", align_bytes=64)
        nc.vector.quantize_mx(
            out=w1_codes[:].bitcast(FP8X4), scales=w1_bytes[:], in_=w1_bf[:].rearrange("p t m j -> p (t m j)")
        )

        x_codes = keep.tile([P, S], U32, name="x_codes", align_bytes=64)
        nc.vector.tensor_copy(x_codes[:], word_table[:].bitcast(U32).indirect(offs_sb[:]))

        def first_product(t, cols, tag):
            bank = psum.tile([P, cols.stop - cols.start], F32, name=f"y_bank{t}_{cols.start}", tag=tag)
            rows = slice(t * P, (t + 1) * P)
            nc.tensor.matmul_mx(
                out=bank[:],
                lhsT=w1_codes[:, rows].bitcast(FP8X4),
                lhsT_scale=w1_bytes[:, rows],
                rhs=x_codes[:, cols].bitcast(FP8X4),
                rhs_scale=x_bytes[:, cols],
                start=True,
                stop=True,
            )
            return bank

        nc.scalar.copy(y_rows[0][:, :HALF], first_product(0, slice(0, HALF), "half_bank0")[:])
        nc.vector.tensor_copy(y_rows[0][:, HALF:S], first_product(0, slice(HALF, S), "half_bank1")[:])
        for t in range(1, PACK):
            nc.vector.tensor_copy(y_rows[t][:, :S], first_product(t, slice(0, S), f"bank{t}")[:])

        w2_src = w2_raw[:].rearrange("p j (m t) -> p m t j", t=PACK)
        w2_codes = keep.tile([P, N], U32, name="w2_codes", align_bytes=64)
        w2_bytes = keep.tile([P, N], U8, name="w2_bytes", align_bytes=64)

        def round_w2(tile, first, t0, t1):
            nc.vector.tensor_copy(
                tile[:, t0 - first : t1 - first].rearrange("p t m j -> p m t j"), w2_src[:, :, t0:t1, :]
            )

        def quantize_w2(tile, first, t0, t1):
            nc.vector.quantize_mx(
                out=w2_codes[:, t0 * P : t1 * P].bitcast(FP8X4),
                scales=w2_bytes[:, t0 * P : t1 * P],
                in_=tile[:, t0 - first : t1 - first].rearrange("p t m j -> p (t m j)"),
            )

        pieces = [(0, 0, S), (1, 0, S), (2, 0, S), (3, 0, S)]
        z_bf = keep.tile([P, 2, PACK, HALF], BF16, name="z_bf")
        z_codes = keep.tile([P, S], U32, name="z_codes", align_bytes=64)
        z_bytes = keep.tile([P, S], U8, name="z_bytes", align_bytes=64)
        members, larger, smaller, gate, diff, z_words = {}, {}, {}, {}, {}, {}

        def piece_tile(kind, n, factor=1, tag=None):
            t, lo, hi = pieces[n]
            return keep.tile([P, factor * (hi - lo)], F32, name=f"{kind}{n}", tag=tag or f"{kind}{n}", align_bytes=64)

        def fetch_members(n, tag=None):
            t, lo, hi = pieces[n]
            members[n] = piece_tile("members", n, 2, tag)
            nc.scalar.activation(members[n][:], y_rows[t][:].indirect(n1_sb[:, lo // 8 : hi // 8]), COPY)

        def maximum(n):
            larger[n] = piece_tile("larger", n)
            nc.vector.tensor_tensor(larger[n][:], members[n][:, 0::2], members[n][:, 1::2], ALU.max)

        def minimum(n):
            smaller[n] = piece_tile("smaller", n)
            nc.vector.tensor_tensor(smaller[n][:], members[n][:, 0::2], members[n][:, 1::2], ALU.min)

        def difference(n):
            t, lo, hi = pieces[n]
            diff[n] = piece_tile("diff", n)
            nc.vector.tensor_tensor(diff[n][:], y_rows[t][:, lo:hi], smaller[n][:], ALU.subtract)

        def sigmoid(n):
            gate[n] = piece_tile("gate", n)
            nc.scalar.activation(gate[n][:], larger[n][:], SIGMOID)

        def product(n, lo=0, hi=S):
            t = n
            nc.vector.scalar_tensor_tensor(
                z_bf[:, lo // HALF : hi // HALF, t, :],
                diff[n][:, lo:hi].rearrange("p (c j) -> p c j", j=HALF),
                gain[:, t : t + 1],
                gate[n][:, lo:hi].rearrange("p (c j) -> p c j", j=HALF),
                ALU.mult,
                ALU.mult,
            )

        def interleave_z(c, copy, tag):
            z_words[c] = keep.tile([P, HALF, PACK], BF16, name=f"z_words{c}", tag=tag, align_bytes=64)
            copy(z_words[c][:].rearrange("p (g i) t -> p g t i", i=4), z_bf[:, c].rearrange("p t (g i) -> p g t i", i=4))

        def quantize_z(c):
            cols = slice(c * HALF, (c + 1) * HALF)
            nc.vector.quantize_mx(
                out=z_codes[:, cols].bitcast(FP8X4), scales=z_bytes[:, cols], in_=z_words[c][:].rearrange("p j t -> p (j t)")
            )

        def second_product(t, cols, tag):
            bank = psum.tile([P, cols.stop - cols.start], F32, name=f"h_bank{t}_{cols.start}", tag=tag)
            rows = slice(t * P, (t + 1) * P)
            nc.tensor.matmul_mx(
                out=bank[:],
                lhsT=w2_codes[:, rows].bitcast(FP8X4),
                lhsT_scale=w2_bytes[:, rows],
                rhs=z_codes[:, cols].bitcast(FP8X4),
                rhs_scale=z_bytes[:, cols],
                start=True,
                stop=True,
            )
            return bank

        fetch_members(0)
        fetch_members(1)
        w2_first = keep.tile([P, 1, P, PACK], BF16, name="w2_first", align_bytes=64)
        round_w2(w2_first, 0, 0, 1)
        maximum(0)
        minimum(0)
        quantize_w2(w2_first, 0, 0, 1)
        difference(0)
        sigmoid(0)
        fetch_members(2, "members0")
        maximum(1)
        minimum(1)
        product(0)
        difference(1)
        sigmoid(1)
        fetch_members(3, "members1")
        maximum(2)
        minimum(2)
        product(1)
        difference(2)
        sigmoid(2)
        minimum(3)
        maximum(3)
        sigmoid(3)
        difference(3)
        product(2)
        product(3, 0, HALF)
        product(3, HALF, S)
        interleave_z(0, nc.vector.tensor_copy, "z_words0")
        interleave_z(1, nc.scalar.copy, "z_words1")
        quantize_z(0)
        bank = second_product(0, slice(0, HALF), "half_bank0")
        nc.scalar.copy(h_rows[0][:, :HALF], bank[:])
        quantize_z(1)
        bank = second_product(0, slice(HALF, S), "half_bank1")
        nc.scalar.copy(h_rows[0][:, HALF:S], bank[:])
        w2_rest = keep.tile([P, PACK - 1, P, PACK], BF16, name="w2_rest", tag="z_words1", align_bytes=64)
        round_w2(w2_rest, 1, 1, 2)
        for t in range(1, PACK):
            if t + 1 < PACK:
                round_w2(w2_rest, 1, t + 1, t + 2)
            quantize_w2(w2_rest, 1, t, t + 1)
            bank = second_product(t, slice(0, S), f"bank{t}")
            nc.vector.tensor_copy(h_rows[t][:, :S], bank[:])

        out_rows = out.rearrange("(p t) j -> p t j", t=PACK)
        for t in range(PACK):
            fetched = keep.tile([P, 3, S], F32, name=f"fetched{t}")
            first = keep.tile([P, S], F32, name=f"first{t}")
            second = keep.tile([P, S], F32, name=f"second{t}")
            result = keep.tile([P, S], F32, name=f"result{t}")
            nc.scalar.activation(fetched[:, 0, :], h_rows[t][:].indirect(n2_sb[:]), COPY)
            nc.scalar.activation(fetched[:, 1, :], h_rows[t][:].indirect(n3_sb[:]), COPY)
            nc.vector.tensor_tensor(first[:], fetched[:, 0, :], h_rows[t][:, :S], ALU.max)
            parts = 2 if t == PACK - 1 else 1
            width = S // parts
            for piece in range(parts):
                cols = slice(piece * width, (piece + 1) * width)
                places = n4_sb[:, cols.start // 16 : cols.stop // 16]
                nc.scalar.activation(fetched[:, 2, cols], h_rows[t][:].indirect(places), COPY)
                runs = [slice(cols.start + r * width // parts, cols.start + (r + 1) * width // parts) for r in range(parts)]
                for run in runs:
                    nc.vector.tensor_tensor(second[:, run], fetched[:, 1, run], fetched[:, 2, run], ALU.max)
                for run in runs:
                    nc.vector.tensor_tensor(result[:, run], first[:, run], second[:, run], ALU.subtract)
                nc.sync.dma_start(out_rows[:, t, cols], result[:, cols])
